import numpy as np
import ml_dtypes


def mxq(x, axis, fmt="e4m3"):
    dtype, down = {"e4m3": (ml_dtypes.float8_e4m3fn, 7), "e5m2": (ml_dtypes.float8_e5m2, 14)}[fmt]
    v = np.moveaxis(np.asarray(x, np.float32).astype(ml_dtypes.bfloat16).astype(np.float64), axis, -1)
    blocks = v.reshape(v.shape[:-1] + (-1, 32))
    amax = np.abs(blocks).max(-1, keepdims=True)
    byte = np.maximum(np.where(amax > 0, np.frexp(amax)[1] - 1 + 127, 0) - down, 1)
    scale = np.exp2(byte - 127.0)
    codes = (blocks / scale).astype(np.float32).astype(dtype).astype(np.float64)
    return np.moveaxis((codes * scale).reshape(v.shape), -1, axis)


WIDE = False


def mx_kscale(k):
    if not WIDE:
        return np.ones(k)
    levels = np.array([10, -10, 5, -5, 0])
    if k % 512:
        return np.exp2(np.random.permutation(np.resize(levels, k // 32))).repeat(32)
    a = np.empty((k // 512, 16))
    for p in range(k // 512):
        a[p, :8] = np.random.permutation(np.resize(levels, 8))
        for g in range(8):
            far = levels[np.abs(levels - a[p, g]) >= 10]
            a[p, g + 8] = far[np.random.randint(len(far))]
    return np.exp2(a.ravel()).repeat(32)


BF16 = ml_dtypes.bfloat16


def bf(x):
    return np.asarray(x, np.float32).astype(BF16)


def f64(x):
    return np.asarray(x).astype(np.float64)


E2M1 = np.array([0.0, 0.5, 1.0, 1.5, 2.0, 3.0, 4.0, 6.0, -0.0, -0.5, -1.0, -1.5, -2.0, -3.0, -4.0, -6.0])


def pack_weight(w, fmt):
    k, n = w.shape
    w = f64(bf(w)).reshape(k // 32, 32, n)
    amax = np.abs(w).max(1)
    if fmt == "e4m3":
        byte = np.frexp(amax)[1] - 1 + 127 - 7
    else:
        mant, ex = np.frexp(amax / 6.0)
        byte = np.where(mant > 0.5, ex, ex - 1) + 127
    byte = np.clip(np.where(amax > 0, byte, 1), 1, 254)
    scaled = (w * np.exp2(127.0 - byte)[:, None, :]).reshape(k, n).astype(np.float32)
    by_word = np.ascontiguousarray(scaled.reshape(k // 512, 128, 4, n).transpose(0, 1, 3, 2))
    if fmt == "e4m3":
        words = by_word.astype(ml_dtypes.float8_e4m3fn).view(np.uint8)
    else:
        c = by_word.astype(ml_dtypes.float4_e2m1fn).view(np.uint8) & 0xF
        words = c[..., 0::2] | (c[..., 1::2] << 4)
    return np.ascontiguousarray(words), np.ascontiguousarray(byte.astype(np.uint8).reshape(k // 512, 16, n))


def unpack_weight(words, scales, fmt):
    g, p, n, _ = words.shape
    if fmt == "e4m3":
        vals = np.ascontiguousarray(words).view(ml_dtypes.float8_e4m3fn).astype(np.float64)
    else:
        nib = np.empty((g, p, n, 4), np.uint8)
        nib[..., 0::2] = words & 0xF
        nib[..., 1::2] = words >> 4
        vals = E2M1[nib]
    vals = vals * np.repeat(np.exp2(scales.astype(np.float64) - 127.0), 8, axis=1)[..., None]
    return vals.transpose(0, 1, 3, 2).reshape(g * 512, n)
def pack4(w):
    words, scales = pack_weight(w, "e2m1")
    return words.reshape(words.shape[0], 128, -1), scales


def unpack4(words, scales):
    return unpack_weight(words.reshape(words.shape[0], 128, -1, 2), scales, "e2m1")


E4M3FN = np.array([(-1.0 if i & 128 else 1.0) * ((1.0 + (i & 7) / 8.0) * 2.0 ** (((i >> 3) & 15) - 7) if i & 120 else (i & 7) * 2.0 ** -9) for i in range(256)])


def e4m3fn_bytes(y):
    return np.clip(np.asarray(y, np.float64), -448.0, 448.0).astype(np.float32).astype(ml_dtypes.float8_e4m3fn).view(np.uint8)


def e4m3fn_values(b):
    return E4M3FN[b]


N, O, V, B = 2048, 512, 1536, 128
FMAX = 448.0


def setup_inputs():
    s = mx_kscale(N)
    c = np.random.standard_normal((O, N)) / np.sqrt(N) * s
    c_scale = (np.abs(c).reshape(O, N // B, B).max(axis=2) / FMAX).astype(np.float32)
    c_bytes = e4m3fn_bytes(c / np.repeat(f64(c_scale), B, axis=1))
    a = np.random.standard_normal((N, N))
    fock = (a + a.T) / np.sqrt(2.0)
    v = np.random.standard_normal((N, V)) / np.sqrt(N) * s[:, None]
    v_words, v_scales = pack4(v)
    return {"c_bytes": c_bytes,
            "c_scale": c_scale,
            "fock": bf(fock / s[:, None] / s),
            "occ": bf(np.random.uniform(0.5, 2.0, (O,))),
            "v_words": v_words,
            "v_scales": v_scales}


def reference(c_bytes, c_scale, fock, occ, v_words, v_scales):
    c = e4m3fn_values(c_bytes) * np.repeat(f64(c_scale), B, axis=1)
    cq = mxq(c, 1, "e4m3")
    half = (cq @ mxq(f64(fock), 0, "e4m3")) * f64(occ)[:, None]
    hq = mxq(half, 1, "e4m3")
    f_oo = hq @ cq.T
    f_ov = hq @ unpack4(v_words, v_scales)
    return f_oo, f_ov

@@ -1,0 +1,264 @@
+from contextlib import ExitStack
+
+import concourse.mybir as mybir
+from concourse.masks import make_identity
+
+F32 = mybir.dt.float32
+BF16 = mybir.dt.bfloat16
+I32 = mybir.dt.int32
+U32 = mybir.dt.uint32
+U8 = mybir.dt.uint8
+FP8 = mybir.dt.float8_e4m3fn
+FP8X4 = mybir.dt.float8_e4m3fn_x4
+FP4X4 = mybir.dt.float4_e2m1fn_x4
+COPY = mybir.ActivationFunctionType.Copy
+MULT = mybir.AluOpType.mult
+
+P = 128
+N, O, V = 2048, 512, 1536
+G = N // 512
+OT = O // P
+B = 128
+
+FLOPS = 2 * O * N * N + 2 * O * N * (O + V)
+
+
+def tile_fock_orbital_blocks_d4_kernel(tc, c_bytes, c_scale, fock, occ, v_words, v_scales, f_oo, f_ov):
+    nc = tc.nc
+    with ExitStack() as ctx:
+        keep = ctx.enter_context(tc.tile_pool(name="keep", bufs=1))
+        raw_pool = ctx.enter_context(tc.tile_pool(name="raw", bufs=12))
+        grp_pool = ctx.enter_context(tc.tile_pool(name="grp", bufs=5))
+        code_pool = ctx.enter_context(tc.tile_pool(name="code", bufs=12))
+        half_pool = ctx.enter_context(tc.tile_pool(name="half", bufs=2))
+        out_pool = ctx.enter_context(tc.tile_pool(name="outs", bufs=8))
+        psum = ctx.enter_context(tc.psum_pool(name="psum", bufs=1))
+
+        def bank(i):
+            return psum.tile([P, 512], F32, name=f"bank{i}", tag=f"bank{i}")
+
+        ident = keep.tile([P, P], F32, name="ident")
+        scale_sb = keep.tile([P, OT, N // B], F32, name="scale_sb")
+        occ_sb = keep.tile([P, O], BF16, name="occ_sb")
+        c_raw = [keep.tile([P, N], U8, name=f"c_raw{a}") for a in range(OT)]
+        c_wide = keep.tile([P, OT, N], BF16, name="c_wide", align_bytes=64)
+        c_grp = keep.tile([P, G, O, 4], BF16, name="c_grp", align_bytes=64)
+        c_codes = keep.tile([P, G, O], U32, name="c_codes", align_bytes=64)
+        c_planes = keep.tile([P, G, O], U8, name="c_planes", align_bytes=64)
+        h_codes = keep.tile([P, G, O], U32, name="h_codes", align_bytes=64)
+        h_planes = keep.tile([P, G, O], U8, name="h_planes", align_bytes=64)
+        v_sb = keep.tile([P, G, 2 * V], U8, name="v_sb", align_bytes=64)
+        v_planes = keep.tile([P, G, V], U8, name="v_planes", align_bytes=64)
+
+        ctx.enter_context(tc.manual_schedule())
+
+        nc.scalar.dma_start(out=scale_sb[:], in_=c_scale.rearrange("(a p) b -> p a b", p=P))
+        for a in range(OT):
+            nc.sync.dma_start(out=c_raw[a][:], in_=c_bytes[a * P : (a + 1) * P, :])
+        make_identity(nc, ident[:])
+        nc.gpsimd.memset(v_planes[:].rearrange("p g n -> p (g n)").bitcast(U32), 0)
+        raws = {}
+
+        def load_fock(g):
+            for k in range(G):
+                raw = raw_pool.tile([P, 4, 512], BF16, name="raw")
+                nc.sync.dma_start(
+                    out=raw[:],
+                    in_=fock[k * 512 : (k + 1) * 512, g * 512 : (g + 1) * 512].rearrange("(p j) n -> p j n", j=4),
+                )
+                raws[g, k] = raw
+
+        load_fock(0)
+        nc.sync.dma_start(out=occ_sb[:], in_=occ.partition_broadcast(P))
+        load_fock(1)
+        for q in range(4):
+            nc.sync.dma_start(
+                out=v_planes[32 * q : 32 * q + 4, :, :].bitcast(I32),
+                in_=v_scales[:, 4 * q : 4 * q + 4, :].rearrange("g r n -> r g n").bitcast(I32),
+            )
+        nc.sync.dma_start(out=v_sb[:].bitcast(I32), in_=v_words.rearrange("g p n -> p g n").bitcast(I32))
+        load_fock(2)
+        load_fock(3)
+
+        def widen(a):
+            for b in range(N // B):
+                src = c_raw[a][:, b * B : (b + 1) * B].bitcast(FP8)
+                dst = c_wide[:, a, b * B : (b + 1) * B]
+                if b % 8 in (0, 3, 6):
+                    nc.scalar.activation(dst, src, COPY, scale=scale_sb[:, a, b : b + 1])
+                else:
+                    nc.vector.tensor_scalar(dst, src, scale_sb[:, a, b : b + 1], None, MULT)
+
+        turned = {}
+
+        def turn(a):
+            words = c_wide[:, a, :].bitcast(F32)
+            for h in range(2):
+                xt = bank(2 * a + h)
+                for gi in range(2):
+                    for u in range(2):
+                        g = 2 * h + gi
+                        col = 256 * gi + 128 * u
+                        nc.tensor.transpose(xt[:, col : col + P], words[:, 256 * g + u : 256 * (g + 1) : 2], ident[:])
+                turned[a, h] = xt
+
+        def untangle(a):
+            for h in range(2):
+                out = c_grp[:, 2 * h : 2 * h + 2, a * P : (a + 1) * P, :].rearrange("p g r j -> p g (r j)").bitcast(F32)
+                out = out.rearrange("p g (r u) -> p g r u", u=2)
+                in_ = turned[a, h][:].rearrange("p (g u r) -> p g r u", g=2, u=2)
+                if h == 0:
+                    nc.vector.tensor_copy(out=out, in_=in_)
+                else:
+                    nc.scalar.copy(out, in_)
+
+        def quantise_c(g):
+            nc.vector.quantize_mx(
+                out=c_codes[:, g, :].bitcast(FP8X4),
+                scales=c_planes[:, g, :],
+                in_=c_grp[:, g, :, :].rearrange("p o j -> p (o j)"),
+            )
+
+        grps, f_codes, f_planes = {}, {}, {}
+
+        def interleave(s):
+            g, k = divmod(s, 4)
+            grp = grp_pool.tile([P, 4, P, 4], BF16, name="grp", align_bytes=64)
+            src = raws[g, k][:].rearrange("p j (m t) -> p t m j", t=4)
+            cut = 2 if s < 6 or k == 3 else 3
+            nc.scalar.copy(grp[:, :cut], src[:, :cut])
+            nc.vector.tensor_copy(out=grp[:, cut:], in_=src[:, cut:])
+            grps[s] = grp
+
+        def quantise_fock(s):
+            codes = code_pool.tile([P, 512], U32, name="f_codes", align_bytes=64)
+            planes = code_pool.tile([P, 512], U8, name="f_planes", align_bytes=64)
+            nc.vector.quantize_mx(
+                out=codes[:].bitcast(FP8X4), scales=planes[:], in_=grps[s][:].rearrange("p t m j -> p (t m j)")
+            )
+            f_codes[s], f_planes[s] = codes, planes
+
+        s1_banks, h_grp = {}, {}
+
+        def stage1(i):
+            g, a = divmod(i, OT)
+            acc = bank(i % 2)
+            for t in range(4):
+                for k in range(G):
+                    nc.tensor.matmul_mx(
+                        out=acc[:, t * P : (t + 1) * P],
+                        lhsT=f_codes[4 * g + k][:, t * P : (t + 1) * P].bitcast(FP8X4),
+                        lhsT_scale=f_planes[4 * g + k][:, t * P : (t + 1) * P],
+                        rhs=c_codes[:, k, a * P : (a + 1) * P].bitcast(FP8X4),
+                        rhs_scale=c_planes[:, k, a * P : (a + 1) * P],
+                        start=(k == 0),
+                        stop=(k == G - 1),
+                    )
+            s1_banks[i] = acc
+
+        def weigh(i):
+            g, a = divmod(i, OT)
+            if a == 0:
+                h_grp[g] = half_pool.tile([P, O, 4], BF16, name="h_grp", align_bytes=64)
+            nc.vector.tensor_tensor(
+                out=h_grp[g][:, a * P : (a + 1) * P, :],
+                in0=s1_banks[i][:].rearrange("p (t o) -> p o t", t=4),
+                in1=occ_sb[:, a * P : (a + 1) * P].unsqueeze(2).to_broadcast([P, P, 4]),
+                op=MULT,
+            )
+
+        def quantise_half(i):
+            g, a = divmod(i, OT)
+            cols = slice(a * P, (a + 1) * P)
+            nc.vector.quantize_mx(
+                out=h_codes[:, g, cols].bitcast(FP8X4),
+                scales=h_planes[:, g, cols],
+                in_=h_grp[g][:, cols, :].rearrange("p o j -> p (o j)"),
+            )
+
+        def pass2(acc, g, a, n, start, stop):
+            if n == 0:
+                rhs, rhs_scale = c_codes[:, g, :].bitcast(FP8X4), c_planes[:, g, :]
+            else:
+                rhs = v_sb[:, g, (n - 1) * 1024 : n * 1024].bitcast(FP4X4)
+                rhs_scale = v_planes[:, g, (n - 1) * 512 : n * 512]
+            nc.tensor.matmul_mx(
+                out=acc[:],
+                lhsT=h_codes[:, g, a * P : (a + 1) * P].bitcast(FP8X4),
+                lhsT_scale=h_planes[:, g, a * P : (a + 1) * P],
+                rhs=rhs,
+                rhs_scale=rhs_scale,
+                start=start,
+                stop=stop,
+            )
+
+        early = [(a, 0) for a in range(OT)] + [(0, 1), (1, 1)]
+        early_acc = {}
+
+        def stage2(i):
+            g, a = divmod(i, OT)
+            for e, (ea, en) in enumerate(early):
+                if ea == a:
+                    if g == 0:
+                        early_acc[e] = bank(2 + e)
+                    pass2(early_acc[e], g, ea, en, g == 0, g == G - 1)
+
+        flip = [0]
+
+        def store(acc, a, n):
+            res = out_pool.tile([P, 512], F32, name="res")
+            if flip[0] % 2 == 0:
+                nc.vector.tensor_copy(out=res[:], in_=acc[:])
+            else:
+                nc.scalar.copy(res[:], acc[:])
+            flip[0] += 1
+            rows = slice(a * P, (a + 1) * P)
+            dst = f_oo[rows, :] if n == 0 else f_ov[rows, (n - 1) * 512 : n * 512]
+            nc.sync.dma_start(out=dst, in_=res[:])
+
+        widen(0)
+        turn(0)
+        widen(1)
+        turn(1)
+        untangle(0)
+        widen(2)
+        turn(2)
+        untangle(1)
+        widen(3)
+        turn(3)
+        untangle(2)
+        interleave(0)
+        untangle(3)
+        for g in range(G):
+            quantise_c(g)
+
+        last = 4 * G
+        for s in range(1, last + 6):
+            if 0 <= s - 6 < last:
+                weigh(s - 6)
+            if s < last:
+                interleave(s)
+            if s - 1 < last:
+                quantise_fock(s - 1)
+            if 0 <= s - 6 < last:
+                quantise_half(s - 6)
+            if 0 <= s - 5 < last:
+                stage1(s - 5)
+            if 0 <= s - 7 < last:
+                stage2(s - 7)
+        late = [(a, n) for n in range(1, 4) for a in range(OT) if (a, n) not in early]
+        order = [0]
+        acc = bank(0)
+        a, n = late[0]
+        for g in range(G - 1):
+            pass2(acc, g, a, n, g == 0, False)
+        stage2(last - 1)
+        pass2(acc, G - 1, a, n, False, True)
+        for e, (ea, en) in enumerate(early):
+            store(early_acc[e], ea, en)
+        store(acc, a, n)
+        for j, (a, n) in enumerate(late[1:]):
+            acc = bank((j + 1) % 8)
+            for g in range(G):
+                pass2(acc, g, a, n, g == 0, g == G - 1)
+            store(acc, a, n)

@@ -20,6 +20,8 @@ G = N // 512
 OT = O // P
 B = 128
 
+SPLIT = (72, 84, 88, 92)
+
 FLOPS = 2 * O * N * N + 2 * O * N * (O + V)
 
 
@@ -27,9 +29,9 @@ def tile_fock_orbital_blocks_d4_kernel(tc, c_bytes, c_scale, fock, occ, v_words,
     nc = tc.nc
     with ExitStack() as ctx:
         keep = ctx.enter_context(tc.tile_pool(name="keep", bufs=1))
-        raw_pool = ctx.enter_context(tc.tile_pool(name="raw", bufs=12))
+        raw_pool = ctx.enter_context(tc.tile_pool(name="raw", bufs=16))
         grp_pool = ctx.enter_context(tc.tile_pool(name="grp", bufs=5))
-        code_pool = ctx.enter_context(tc.tile_pool(name="code", bufs=12))
+        code_pool = ctx.enter_context(tc.tile_pool(name="code", bufs=10))
         half_pool = ctx.enter_context(tc.tile_pool(name="half", bufs=2))
         out_pool = ctx.enter_context(tc.tile_pool(name="outs", bufs=8))
         psum = ctx.enter_context(tc.psum_pool(name="psum", bufs=1))
@@ -68,14 +70,14 @@ def tile_fock_orbital_blocks_d4_kernel(tc, c_bytes, c_scale, fock, occ, v_words,
                 )
                 raws[g, k] = raw
 
-        load_fock(0)
-        nc.sync.dma_start(out=occ_sb[:], in_=occ.partition_broadcast(P))
-        load_fock(1)
+        nc.gpsimd.dma_start(out=occ_sb[:], in_=occ.partition_broadcast(P))
         for q in range(4):
-            nc.sync.dma_start(
+            nc.gpsimd.dma_start(
                 out=v_planes[32 * q : 32 * q + 4, :, :].bitcast(I32),
                 in_=v_scales[:, 4 * q : 4 * q + 4, :].rearrange("g r n -> r g n").bitcast(I32),
             )
+        load_fock(0)
+        load_fock(1)
         nc.sync.dma_start(out=v_sb[:].bitcast(I32), in_=v_words.rearrange("g p n -> p g n").bitcast(I32))
         load_fock(2)
         load_fock(3)
@@ -124,10 +126,11 @@ def tile_fock_orbital_blocks_d4_kernel(tc, c_bytes, c_scale, fock, occ, v_words,
         def interleave(s):
             g, k = divmod(s, 4)
             grp = grp_pool.tile([P, 4, P, 4], BF16, name="grp", align_bytes=64)
-            src = raws[g, k][:].rearrange("p j (m t) -> p t m j", t=4)
-            cut = 2 if s < 6 or k == 3 else 3
-            nc.scalar.copy(grp[:, :cut], src[:, :cut])
-            nc.vector.tensor_copy(out=grp[:, cut:], in_=src[:, cut:])
+            src = raws[g, k][:].rearrange("p j (m t) -> p m j t", t=4)
+            dst = grp[:].rearrange("p t m j -> p m j t")
+            cut = SPLIT[g]
+            nc.scalar.copy(dst[:, :cut], src[:, :cut])
+            nc.vector.tensor_copy(out=dst[:, cut:], in_=src[:, cut:])
             grps[s] = grp
 
         def quantise_fock(s):
@@ -235,15 +238,15 @@ def tile_fock_orbital_blocks_d4_kernel(tc, c_bytes, c_scale, fock, occ, v_words,
         last = 4 * G
         for s in range(1, last + 6):
             if 0 <= s - 6 < last:
-                weigh(s - 6)
+                quantise_half(s - 6)
             if s < last:
                 interleave(s)
             if s - 1 < last:
                 quantise_fock(s - 1)
-            if 0 <= s - 6 < last:
-                quantise_half(s - 6)
+            if 0 <= s - 4 < last:
+                stage1(s - 4)
             if 0 <= s - 5 < last:
-                stage1(s - 5)
+                weigh(s - 5)
             if 0 <= s - 7 < last:
                 stage2(s - 7)
         late = [(a, n) for n in range(1, 4) for a in range(OT) if (a, n) not in early]

@@ -20,7 +20,9 @@ G = N // 512
 OT = O // P
 B = 128
 
-SPLIT = (72, 84, 88, 92)
+SPLIT = (64,) * 4 + (76,) * 4 + (92,) * 4 + (100,) * 4
+WIDEN_S = (6, 6, 6, 6)
+UNTANGLE_V = ((0, 0), (1, 0), (2, 0), (3, 0))
 
 FLOPS = 2 * O * N * N + 2 * O * N * (O + V)
 
@@ -70,14 +72,14 @@ def tile_fock_orbital_blocks_d4_kernel(tc, c_bytes, c_scale, fock, occ, v_words,
                 )
                 raws[g, k] = raw
 
-        nc.gpsimd.dma_start(out=occ_sb[:], in_=occ.partition_broadcast(P))
+        load_fock(0)
+        nc.sync.dma_start(out=occ_sb[:], in_=occ.partition_broadcast(P))
+        load_fock(1)
         for q in range(4):
-            nc.gpsimd.dma_start(
+            nc.sync.dma_start(
                 out=v_planes[32 * q : 32 * q + 4, :, :].bitcast(I32),
                 in_=v_scales[:, 4 * q : 4 * q + 4, :].rearrange("g r n -> r g n").bitcast(I32),
             )
-        load_fock(0)
-        load_fock(1)
         nc.sync.dma_start(out=v_sb[:].bitcast(I32), in_=v_words.rearrange("g p n -> p g n").bitcast(I32))
         load_fock(2)
         load_fock(3)
@@ -86,7 +88,7 @@ def tile_fock_orbital_blocks_d4_kernel(tc, c_bytes, c_scale, fock, occ, v_words,
             for b in range(N // B):
                 src = c_raw[a][:, b * B : (b + 1) * B].bitcast(FP8)
                 dst = c_wide[:, a, b * B : (b + 1) * B]
-                if b % 8 in (0, 3, 6):
+                if b * WIDEN_S[a] // 16 != (b + 1) * WIDEN_S[a] // 16:
                     nc.scalar.activation(dst, src, COPY, scale=scale_sb[:, a, b : b + 1])
                 else:
                     nc.vector.tensor_scalar(dst, src, scale_sb[:, a, b : b + 1], None, MULT)
@@ -109,7 +111,7 @@ def tile_fock_orbital_blocks_d4_kernel(tc, c_bytes, c_scale, fock, occ, v_words,
                 out = c_grp[:, 2 * h : 2 * h + 2, a * P : (a + 1) * P, :].rearrange("p g r j -> p g (r j)").bitcast(F32)
                 out = out.rearrange("p g (r u) -> p g r u", u=2)
                 in_ = turned[a, h][:].rearrange("p (g u r) -> p g r u", g=2, u=2)
-                if h == 0:
+                if (a, h) in UNTANGLE_V:
                     nc.vector.tensor_copy(out=out, in_=in_)
                 else:
                     nc.scalar.copy(out, in_)
@@ -128,7 +130,7 @@ def tile_fock_orbital_blocks_d4_kernel(tc, c_bytes, c_scale, fock, occ, v_words,
             grp = grp_pool.tile([P, 4, P, 4], BF16, name="grp", align_bytes=64)
             src = raws[g, k][:].rearrange("p j (m t) -> p m j t", t=4)
             dst = grp[:].rearrange("p t m j -> p m j t")
-            cut = SPLIT[g]
+            cut = SPLIT[s]
             nc.scalar.copy(dst[:, :cut], src[:, :cut])
             nc.vector.tensor_copy(out=dst[:, cut:], in_=src[:, cut:])
             grps[s] = grp
@@ -179,14 +181,14 @@ def tile_fock_orbital_blocks_d4_kernel(tc, c_bytes, c_scale, fock, occ, v_words,
                 in_=h_grp[g][:, cols, :].rearrange("p o j -> p (o j)"),
             )
 
-        def pass2(acc, g, a, n, start, stop):
+        def pass2(acc, g, a, n, start, stop, cols=slice(0, 512)):
             if n == 0:
-                rhs, rhs_scale = c_codes[:, g, :].bitcast(FP8X4), c_planes[:, g, :]
+                rhs, rhs_scale = c_codes[:, g, cols].bitcast(FP8X4), c_planes[:, g, cols]
             else:
                 rhs = v_sb[:, g, (n - 1) * 1024 : n * 1024].bitcast(FP4X4)
                 rhs_scale = v_planes[:, g, (n - 1) * 512 : n * 512]
             nc.tensor.matmul_mx(
-                out=acc[:],
+                out=acc,
                 lhsT=h_codes[:, g, a * P : (a + 1) * P].bitcast(FP8X4),
                 lhsT_scale=h_planes[:, g, a * P : (a + 1) * P],
                 rhs=rhs,
@@ -195,7 +197,7 @@ def tile_fock_orbital_blocks_d4_kernel(tc, c_bytes, c_scale, fock, occ, v_words,
                 stop=stop,
             )
 
-        early = [(a, 0) for a in range(OT)] + [(0, 1), (1, 1)]
+        early = [(a, 0) for a in range(3)] + [(a, 1) for a in range(3)]
         early_acc = {}
 
         def stage2(i):
@@ -204,20 +206,21 @@ def tile_fock_orbital_blocks_d4_kernel(tc, c_bytes, c_scale, fock, occ, v_words,
                 if ea == a:
                     if g == 0:
                         early_acc[e] = bank(2 + e)
-                    pass2(early_acc[e], g, ea, en, g == 0, g == G - 1)
+                    pass2(early_acc[e][:], g, ea, en, g == 0, g == G - 1)
 
         flip = [0]
 
-        def store(acc, a, n):
-            res = out_pool.tile([P, 512], F32, name="res")
+        def store(acc, a, n, cols=slice(0, 512)):
+            res = out_pool.tile([P, 512], F32, name="res")[:, cols]
+            acc = acc[:, cols]
             if flip[0] % 2 == 0:
-                nc.vector.tensor_copy(out=res[:], in_=acc[:])
+                nc.vector.tensor_copy(out=res, in_=acc)
             else:
-                nc.scalar.copy(res[:], acc[:])
+                nc.scalar.copy(res, acc)
             flip[0] += 1
             rows = slice(a * P, (a + 1) * P)
-            dst = f_oo[rows, :] if n == 0 else f_ov[rows, (n - 1) * 512 : n * 512]
-            nc.sync.dma_start(out=dst, in_=res[:])
+            dst = f_oo[rows, cols] if n == 0 else f_ov[rows, (n - 1) * 512 : n * 512]
+            nc.sync.dma_start(out=dst, in_=res)
 
         widen(0)
         turn(0)
@@ -249,19 +252,24 @@ def tile_fock_orbital_blocks_d4_kernel(tc, c_bytes, c_scale, fock, occ, v_words,
                 weigh(s - 5)
             if 0 <= s - 7 < last:
                 stage2(s - 7)
-        late = [(a, n) for n in range(1, 4) for a in range(OT) if (a, n) not in early]
-        order = [0]
+        late = [(a, n) for n in (1, 2, 3) for a in range(OT) if (a, n) not in early]
         acc = bank(0)
         a, n = late[0]
         for g in range(G - 1):
-            pass2(acc, g, a, n, g == 0, False)
+            pass2(acc[:], g, a, n, g == 0, False)
         stage2(last - 1)
-        pass2(acc, G - 1, a, n, False, True)
+        pass2(acc[:], G - 1, a, n, False, True)
         for e, (ea, en) in enumerate(early):
             store(early_acc[e], ea, en)
         store(acc, a, n)
         for j, (a, n) in enumerate(late[1:]):
             acc = bank((j + 1) % 8)
             for g in range(G):
-                pass2(acc, g, a, n, g == 0, g == G - 1)
+                pass2(acc[:], g, a, n, g == 0, g == G - 1)
             store(acc, a, n)
+        for h in range(2):
+            cols = slice(256 * h, 256 * h + 256)
+            acc = bank((len(late) + h) % 8)
+            for g in range(G):
+                pass2(acc[:, cols], g, OT - 1, 0, g == 0, g == G - 1, cols)
+            store(acc, OT - 1, 0, cols)

@@ -166,9 +166,9 @@ def tile_fock_orbital_blocks_d4_kernel(tc, c_bytes, c_scale, fock, occ, v_words,
             if a == 0:
                 h_grp[g] = half_pool.tile([P, O, 4], BF16, name="h_grp", align_bytes=64)
             nc.vector.tensor_tensor(
-                out=h_grp[g][:, a * P : (a + 1) * P, :],
-                in0=s1_banks[i][:].rearrange("p (t o) -> p o t", t=4),
-                in1=occ_sb[:, a * P : (a + 1) * P].unsqueeze(2).to_broadcast([P, P, 4]),
+                out=h_grp[g][:, a * P : (a + 1) * P, :].rearrange("p (b i) t -> p b t i", i=4),
+                in0=s1_banks[i][:].rearrange("p (t b i) -> p b t i", t=4, i=4),
+                in1=occ_sb[:, a * P : (a + 1) * P].rearrange("p (b i) -> p b i", i=4).unsqueeze(2).to_broadcast([P, 32, 4, 4]),
                 op=MULT,
             )
 
@@ -241,15 +241,15 @@ def tile_fock_orbital_blocks_d4_kernel(tc, c_bytes, c_scale, fock, occ, v_words,
         last = 4 * G
         for s in range(1, last + 6):
             if 0 <= s - 6 < last:
-                quantise_half(s - 6)
+                weigh(s - 6)
             if s < last:
                 interleave(s)
             if s - 1 < last:
                 quantise_fock(s - 1)
-            if 0 <= s - 4 < last:
-                stage1(s - 4)
+            if 0 <= s - 6 < last:
+                quantise_half(s - 6)
             if 0 <= s - 5 < last:
-                weigh(s - 5)
+                stage1(s - 5)
             if 0 <= s - 7 < last:
                 stage2(s - 7)
         late = [(a, n) for n in (1, 2, 3) for a in range(OT) if (a, n) not in early]

from contextlib import ExitStack

import concourse.mybir as mybir
from concourse.masks import make_identity

F32 = mybir.dt.float32
BF16 = mybir.dt.bfloat16
I32 = mybir.dt.int32
U32 = mybir.dt.uint32
U8 = mybir.dt.uint8
FP8 = mybir.dt.float8_e4m3fn
FP8X4 = mybir.dt.float8_e4m3fn_x4
FP4X4 = mybir.dt.float4_e2m1fn_x4
COPY = mybir.ActivationFunctionType.Copy
MULT = mybir.AluOpType.mult

P = 128
N, O, V = 2048, 512, 1536
G = N // 512
OT = O // P
B = 128

SPLIT = (64,) * 4 + (76,) * 4 + (92,) * 4 + (100,) * 4
WIDEN_S = (6, 6, 6, 6)
UNTANGLE_V = ((0, 0), (1, 0), (2, 0), (3, 0))

FLOPS = 2 * O * N * N + 2 * O * N * (O + V)


def tile_fock_orbital_blocks_d4_kernel(tc, c_bytes, c_scale, fock, occ, v_words, v_scales, f_oo, f_ov):
    nc = tc.nc
    with ExitStack() as ctx:
        keep = ctx.enter_context(tc.tile_pool(name="keep", bufs=1))
        raw_pool = ctx.enter_context(tc.tile_pool(name="raw", bufs=16))
        grp_pool = ctx.enter_context(tc.tile_pool(name="grp", bufs=5))
        code_pool = ctx.enter_context(tc.tile_pool(name="code", bufs=10))
        half_pool = ctx.enter_context(tc.tile_pool(name="half", bufs=2))
        out_pool = ctx.enter_context(tc.tile_pool(name="outs", bufs=8))
        psum = ctx.enter_context(tc.psum_pool(name="psum", bufs=1))

        def bank(i):
            return psum.tile([P, 512], F32, name=f"bank{i}", tag=f"bank{i}")

        ident = keep.tile([P, P], F32, name="ident")
        scale_sb = keep.tile([P, OT, N // B], F32, name="scale_sb")
        occ_sb = keep.tile([P, O], BF16, name="occ_sb")
        c_raw = [keep.tile([P, N], U8, name=f"c_raw{a}") for a in range(OT)]
        c_wide = keep.tile([P, OT, N], BF16, name="c_wide", align_bytes=64)
        c_grp = keep.tile([P, G, O, 4], BF16, name="c_grp", align_bytes=64)
        c_codes = keep.tile([P, G, O], U32, name="c_codes", align_bytes=64)
        c_planes = keep.tile([P, G, O], U8, name="c_planes", align_bytes=64)
        h_codes = keep.tile([P, G, O], U32, name="h_codes", align_bytes=64)
        h_planes = keep.tile([P, G, O], U8, name="h_planes", align_bytes=64)
        v_sb = keep.tile([P, G, 2 * V], U8, name="v_sb", align_bytes=64)
        v_planes = keep.tile([P, G, V], U8, name="v_planes", align_bytes=64)

        ctx.enter_context(tc.manual_schedule())

        nc.scalar.dma_start(out=scale_sb[:], in_=c_scale.rearrange("(a p) b -> p a b", p=P))
        for a in range(OT):
            nc.sync.dma_start(out=c_raw[a][:], in_=c_bytes[a * P : (a + 1) * P, :])
        make_identity(nc, ident[:])
        nc.gpsimd.memset(v_planes[:].rearrange("p g n -> p (g n)").bitcast(U32), 0)
        raws = {}

        def load_fock(g):
            for k in range(G):
                raw = raw_pool.tile([P, 4, 512], BF16, name="raw")
                nc.sync.dma_start(
                    out=raw[:],
                    in_=fock[k * 512 : (k + 1) * 512, g * 512 : (g + 1) * 512].rearrange("(p j) n -> p j n", j=4),
                )
                raws[g, k] = raw

        load_fock(0)
        nc.sync.dma_start(out=occ_sb[:], in_=occ.partition_broadcast(P))
        load_fock(1)
        for q in range(4):
            nc.sync.dma_start(
                out=v_planes[32 * q : 32 * q + 4, :, :].bitcast(I32),
                in_=v_scales[:, 4 * q : 4 * q + 4, :].rearrange("g r n -> r g n").bitcast(I32),
            )
        nc.sync.dma_start(out=v_sb[:].bitcast(I32), in_=v_words.rearrange("g p n -> p g n").bitcast(I32))
        load_fock(2)
        load_fock(3)

        def widen(a):
            for b in range(N // B):
                src = c_raw[a][:, b * B : (b + 1) * B].bitcast(FP8)
                dst = c_wide[:, a, b * B : (b + 1) * B]
                if b * WIDEN_S[a] // 16 != (b + 1) * WIDEN_S[a] // 16:
                    nc.scalar.activation(dst, src, COPY, scale=scale_sb[:, a, b : b + 1])
                else:
                    nc.vector.tensor_scalar(dst, src, scale_sb[:, a, b : b + 1], None, MULT)

        turned = {}

        def turn(a):
            words = c_wide[:, a, :].bitcast(F32)
            for h in range(2):
                xt = bank(2 * a + h)
                for gi in range(2):
                    for u in range(2):
                        g = 2 * h + gi
                        col = 256 * gi + 128 * u
                        nc.tensor.transpose(xt[:, col : col + P], words[:, 256 * g + u : 256 * (g + 1) : 2], ident[:])
                turned[a, h] = xt

        def untangle(a):
            for h in range(2):
                out = c_grp[:, 2 * h : 2 * h + 2, a * P : (a + 1) * P, :].rearrange("p g r j -> p g (r j)").bitcast(F32)
                out = out.rearrange("p g (r u) -> p g r u", u=2)
                in_ = turned[a, h][:].rearrange("p (g u r) -> p g r u", g=2, u=2)
                if (a, h) in UNTANGLE_V:
                    nc.vector.tensor_copy(out=out, in_=in_)
                else:
                    nc.scalar.copy(out, in_)

        def quantise_c(g):
            nc.vector.quantize_mx(
                out=c_codes[:, g, :].bitcast(FP8X4),
                scales=c_planes[:, g, :],
                in_=c_grp[:, g, :, :].rearrange("p o j -> p (o j)"),
            )

        grps, f_codes, f_planes = {}, {}, {}

        def interleave(s):
            g, k = divmod(s, 4)
            grp = grp_pool.tile([P, 4, P, 4], BF16, name="grp", align_bytes=64)
            src = raws[g, k][:].rearrange("p j (m t) -> p m j t", t=4)
            dst = grp[:].rearrange("p t m j -> p m j t")
            cut = SPLIT[s]
            nc.scalar.copy(dst[:, :cut], src[:, :cut])
            nc.vector.tensor_copy(out=dst[:, cut:], in_=src[:, cut:])
            grps[s] = grp

        def quantise_fock(s):
            codes = code_pool.tile([P, 512], U32, name="f_codes", align_bytes=64)
            planes = code_pool.tile([P, 512], U8, name="f_planes", align_bytes=64)
            nc.vector.quantize_mx(
                out=codes[:].bitcast(FP8X4), scales=planes[:], in_=grps[s][:].rearrange("p t m j -> p (t m j)")
            )
            f_codes[s], f_planes[s] = codes, planes

        s1_banks, h_grp = {}, {}

        def stage1(i):
            g, a = divmod(i, OT)
            acc = bank(i % 2)
            for t in range(4):
                for k in range(G):
                    nc.tensor.matmul_mx(
                        out=acc[:, t * P : (t + 1) * P],
                        lhsT=f_codes[4 * g + k][:, t * P : (t + 1) * P].bitcast(FP8X4),
                        lhsT_scale=f_planes[4 * g + k][:, t * P : (t + 1) * P],
                        rhs=c_codes[:, k, a * P : (a + 1) * P].bitcast(FP8X4),
                        rhs_scale=c_planes[:, k, a * P : (a + 1) * P],
                        start=(k == 0),
                        stop=(k == G - 1),
                    )
            s1_banks[i] = acc

        def weigh(i):
            g, a = divmod(i, OT)
            if a == 0:
                h_grp[g] = half_pool.tile([P, O, 4], BF16, name="h_grp", align_bytes=64)
            nc.vector.tensor_tensor(
                out=h_grp[g][:, a * P : (a + 1) * P, :].rearrange("p (b i) t -> p b t i", i=4),
                in0=s1_banks[i][:].rearrange("p (t b i) -> p b t i", t=4, i=4),
                in1=occ_sb[:, a * P : (a + 1) * P].rearrange("p (b i) -> p b i", i=4).unsqueeze(2).to_broadcast([P, 32, 4, 4]),
                op=MULT,
            )

        def quantise_half(i):
            g, a = divmod(i, OT)
            cols = slice(a * P, (a + 1) * P)
            nc.vector.quantize_mx(
                out=h_codes[:, g, cols].bitcast(FP8X4),
                scales=h_planes[:, g, cols],
                in_=h_grp[g][:, cols, :].rearrange("p o j -> p (o j)"),
            )

        def pass2(acc, g, a, n, start, stop, cols=slice(0, 512)):
            if n == 0:
                rhs, rhs_scale = c_codes[:, g, cols].bitcast(FP8X4), c_planes[:, g, cols]
            else:
                rhs = v_sb[:, g, (n - 1) * 1024 : n * 1024].bitcast(FP4X4)
                rhs_scale = v_planes[:, g, (n - 1) * 512 : n * 512]
            nc.tensor.matmul_mx(
                out=acc,
                lhsT=h_codes[:, g, a * P : (a + 1) * P].bitcast(FP8X4),
                lhsT_scale=h_planes[:, g, a * P : (a + 1) * P],
                rhs=rhs,
                rhs_scale=rhs_scale,
                start=start,
                stop=stop,
            )

        early = [(a, 0) for a in range(3)] + [(a, 1) for a in range(3)]
        early_acc = {}

        def stage2(i):
            g, a = divmod(i, OT)
            for e, (ea, en) in enumerate(early):
                if ea == a:
                    if g == 0:
                        early_acc[e] = bank(2 + e)
                    pass2(early_acc[e][:], g, ea, en, g == 0, g == G - 1)

        flip = [0]

        def store(acc, a, n, cols=slice(0, 512)):
            res = out_pool.tile([P, 512], F32, name="res")[:, cols]
            acc = acc[:, cols]
            if flip[0] % 2 == 0:
                nc.vector.tensor_copy(out=res, in_=acc)
            else:
                nc.scalar.copy(res, acc)
            flip[0] += 1
            rows = slice(a * P, (a + 1) * P)
            dst = f_oo[rows, cols] if n == 0 else f_ov[rows, (n - 1) * 512 : n * 512]
            nc.sync.dma_start(out=dst, in_=res)

        widen(0)
        turn(0)
        widen(1)
        turn(1)
        untangle(0)
        widen(2)
        turn(2)
        untangle(1)
        widen(3)
        turn(3)
        untangle(2)
        interleave(0)
        untangle(3)
        for g in range(G):
            quantise_c(g)

        last = 4 * G
        for s in range(1, last + 6):
            if 0 <= s - 6 < last:
                weigh(s - 6)
            if s < last:
                interleave(s)
            if s - 1 < last:
                quantise_fock(s - 1)
            if 0 <= s - 6 < last:
                quantise_half(s - 6)
            if 0 <= s - 5 < last:
                stage1(s - 5)
            if 0 <= s - 7 < last:
                stage2(s - 7)
        late = [(a, n) for n in (1, 2, 3) for a in range(OT) if (a, n) not in early]
        acc = bank(0)
        a, n = late[0]
        for g in range(G - 1):
            pass2(acc[:], g, a, n, g == 0, False)
        stage2(last - 1)
        pass2(acc[:], G - 1, a, n, False, True)
        for e, (ea, en) in enumerate(early):
            store(early_acc[e], ea, en)
        store(acc, a, n)
        for j, (a, n) in enumerate(late[1:]):
            acc = bank((j + 1) % 8)
            for g in range(G):
                pass2(acc[:], g, a, n, g == 0, g == G - 1)
            store(acc, a, n)
        for h in range(2):
            cols = slice(256 * h, 256 * h + 256)
            acc = bank((len(late) + h) % 8)
            for g in range(G):
                pass2(acc[:, cols], g, OT - 1, 0, g == 0, g == G - 1, cols)
            store(acc, OT - 1, 0, cols)
